import numpy as np
import ml_dtypes


def mxq(x, axis, fmt="e4m3"):
    dtype, down = {"e4m3": (ml_dtypes.float8_e4m3fn, 7), "e5m2": (ml_dtypes.float8_e5m2, 14)}[fmt]
    v = np.moveaxis(np.asarray(x, np.float32).astype(ml_dtypes.bfloat16).astype(np.float64), axis, -1)
    blocks = v.reshape(v.shape[:-1] + (-1, 32))
    amax = np.abs(blocks).max(-1, keepdims=True)
    byte = np.maximum(np.where(amax > 0, np.frexp(amax)[1] - 1 + 127, 0) - down, 1)
    scale = np.exp2(byte - 127.0)
    codes = (blocks / scale).astype(np.float32).astype(dtype).astype(np.float64)
    return np.moveaxis((codes * scale).reshape(v.shape), -1, axis)


WIDE = False


def mx_kscale(k):
    if not WIDE:
        return np.ones(k)
    levels = np.array([10, -10, 5, -5, 0])
    if k % 512:
        return np.exp2(np.random.permutation(np.resize(levels, k // 32))).repeat(32)
    a = np.empty((k // 512, 16))
    for p in range(k // 512):
        a[p, :8] = np.random.permutation(np.resize(levels, 8))
        for g in range(8):
            far = levels[np.abs(levels - a[p, g]) >= 10]
            a[p, g + 8] = far[np.random.randint(len(far))]
    return np.exp2(a.ravel()).repeat(32)


def f64(x):
    return np.asarray(x).astype(np.float64)


def striped(idx):
    return np.tile(idx.reshape(-1, 16).T, (8, 1)).astype(np.uint16)


def unstriped(offs):
    return offs[:16].T.reshape(-1).astype(np.int64)


def striped8(idx):
    return np.concatenate([x.reshape(-1, 16).T for x in idx]).astype(np.uint16)


def runs(offs, k):
    lists = np.stack([offs[16 * r : 16 * r + 16].T.reshape(-1) for r in range(8)]).astype(np.int64)
    return lists[np.arange(k) % 512 // 64]


def pack_weight(w):
    k, n = w.shape
    w = f64(np.asarray(w, np.float32).astype(ml_dtypes.bfloat16)).reshape(k // 32, 32, n)
    amax = np.abs(w).max(1)
    byte = np.clip(np.where(amax > 0, np.frexp(amax)[1] - 1 + 127 - 7, 1), 1, 254)
    scaled = (w * np.exp2(127.0 - byte)[:, None, :]).reshape(k, n).astype(np.float32)
    words = np.ascontiguousarray(scaled.reshape(k // 512, 128, 4, n).transpose(0, 1, 3, 2)).astype(ml_dtypes.float8_e4m3fn).view(np.uint8)
    return words, np.ascontiguousarray(byte.astype(np.uint8).reshape(k // 512, 16, n))


def unpack_weight(words, scales):
    g, p, n, _ = words.shape
    vals = np.ascontiguousarray(words).view(ml_dtypes.float8_e4m3fn).astype(np.float64) * np.repeat(np.exp2(scales.astype(np.float64) - 127.0), 8, axis=1)[..., None]
    return vals.transpose(0, 1, 3, 2).reshape(g * 512, n)


def relu(v):
    return np.maximum(v, 0.0)

def planes(y):
    n, m = y.shape
    v = y.astype(np.float32).astype(ml_dtypes.bfloat16).astype(np.float64).reshape(n // 32, 32, m)
    top = np.abs(v).max(1)
    byte = np.clip(np.where(top > 0, np.frexp(top)[1] - 1 + 127 - 7, 1), 1, 254)
    codes = (v * np.exp2(127.0 - byte)[:, None, :]).reshape(n, m).astype(np.float32).astype(ml_dtypes.float8_e4m3fn).view(np.uint8)
    words = codes.reshape(n // 512, 128, 4, m).transpose(0, 1, 3, 2)
    return np.ascontiguousarray(words), np.ascontiguousarray(byte.astype(np.uint8).reshape(n // 512, 16, m))


K, T, S, G, H, J, W = 512, 2048, 512, 2048, 512, 512, 384


def setup_inputs():
    n = np.random.standard_normal
    s = mx_kscale(K)[:, None]
    u = mx_kscale(S)
    packed_xT = pack_weight(n((K, T)) * s)
    packed_dT = pack_weight(n((K, G)) / s)
    return {
        "x_words": packed_xT[0],
        "x_scales": packed_xT[1],
        "d_words": packed_dT[0],
        "d_scales": packed_dT[1],
        "tab": n((H, J)).astype(np.float32),
        "ga": (np.random.uniform(0.5, 1.5, (H, 1)) * u[:, None]).astype(np.float32),
        "gb": (np.random.uniform(0.5, 1.5, (H, 1)) / u[:, None]).astype(np.float32),
        "offs": striped(np.random.permutation(T)[:S]),
        "kidx": striped8(np.random.randint(0, G, (8, H))),
        "n1": striped8(np.stack([np.random.permutation(S) for _ in range(8)])),
        "n2": striped8(np.random.randint(0, J, (8, S))),
        "n3": striped8(np.stack([np.random.permutation(S) for _ in range(8)])),
        "n4": striped(np.random.permutation(S)[:W]),
        "n5": striped(np.random.permutation(S)[:W]),
    }


def reference(x_words, x_scales, d_words, d_scales, tab, ga, gb, offs, kidx, n1, n2, n3, n4, n5):
    d_kidx = unpack_weight(d_words, d_scales)[np.arange(K)[:, None], runs(kidx, K)]
    xq = unpack_weight(x_words, x_scales)[:, unstriped(offs)]
    s = 0.0625 * (d_kidx.T @ xq)
    rl = relu(s)
    ds = np.zeros((H, S))
    ds[np.arange(H)[:, None], runs(n1, H)] = rl
    z = f64(ga) * (ds - (0.5 * s))
    z2 = f64(gb) * (np.maximum(s + f64(tab)[np.arange(H)[:, None], runs(n2, H)], s[np.arange(H)[:, None], runs(n3, H)]))
    cm = 0.0625 * ((mxq(z, 0, "e4m3").T @ mxq(z2, 0, "e4m3")))
    old = cm[:, unstriped(n4)]
    pa = cm[:, unstriped(n5)]
    ra = old - (0.5 * pa)
    out = cm.copy()
    out[:, unstriped(n4)] = ra
    return (out,) + planes(out)

@@ -1,0 +1,257 @@
+from contextlib import ExitStack
+
+import concourse.mybir as mybir
+
+K, T, S, G, H, J, W = 512, 2048, 512, 2048, 512, 512, 384
+FLOPS = 2 * K * H * S + 2 * H * S * S
+
+F32 = mybir.dt.float32
+BF16 = mybir.dt.bfloat16
+I32 = mybir.dt.int32
+U32 = mybir.dt.uint32
+U16 = mybir.dt.uint16
+U8 = mybir.dt.uint8
+FP8X4 = mybir.dt.float8_e4m3fn_x4
+ALU = mybir.AluOpType
+ACT = mybir.ActivationFunctionType
+
+P = 128
+PACK = 4
+HALF = S // 2
+LIST_HALF = HALF // 16
+
+
+def tile_picked_simksendkindkdif_none_po_kernel(
+    tc, x_words, x_scales, d_words, d_scales, tab, ga, gb, offs, kidx, n1, n2, n3, n4, n5, out_0, out_1, out_2
+):
+    nc = tc.nc
+    with ExitStack() as ctx:
+        keep = ctx.enter_context(tc.tile_pool(name="keep", bufs=1))
+        psum = ctx.enter_context(tc.psum_pool(name="psum", bufs=1))
+
+        def load_list(name, ap):
+            tile = keep.tile(list(ap.shape), U16, name=name)
+            nc.sync.dma_start(tile[:], ap)
+            return tile
+
+        def load_scale_rows(name, ap):
+            tile = keep.tile([P, ap.shape[2]], U8, name=name)
+            rows = ap[0].bitcast(I32)
+            nc.sync.dma_start(tile[:].bitcast(I32), rows.unsqueeze(1).to_broadcast([16, 8, rows.shape[1]]))
+            return tile
+
+        def load_words(name, ap):
+            tile = keep.tile([P, ap.shape[2]], I32, name=name)
+            nc.sync.dma_start(tile[:], ap[0].rearrange("p n t -> p (n t)").bitcast(I32))
+            return tile
+
+        kidx_list = load_list("kidx_list", kidx)
+        d_scale_table = load_scale_rows("d_scale_table", d_scales)
+        offs_list = load_list("offs_list", offs)
+        x_scale_table = load_scale_rows("x_scale_table", x_scales)
+        d_word_table = load_words("d_word_table", d_words)
+        ga_sb = keep.tile([P, PACK], F32, name="ga_sb")
+        gb_sb = keep.tile([P, PACK], F32, name="gb_sb")
+        nc.sync.dma_start(gb_sb[:], gb.rearrange("(p t) o -> p (t o)", t=PACK))
+        nc.sync.dma_start(ga_sb[:], ga.rearrange("(p t) o -> p (t o)", t=PACK))
+        n1_list = load_list("n1_list", n1)
+        n3_list = load_list("n3_list", n3)
+        n2_list = load_list("n2_list", n2)
+        n4_list = load_list("n4_list", n4)
+        x_word_table = load_words("x_word_table", x_words)
+        n5_list = load_list("n5_list", n5)
+        tab_rows = tab.rearrange("(p t) c -> p t c", t=PACK)
+        tab_sb = {}
+
+        def load_tab(t, tag):
+            tab_sb[t] = keep.tile([P, J], F32, name="tab%d" % t, tag=tag)
+            nc.sync.dma_start(tab_sb[t][:], tab_rows[:, t, :])
+
+        load_tab(0, "tab0")
+        load_tab(1, "tab1")
+
+        d_bytes = keep.tile([P, H], U8, name="d_bytes")
+        x_bytes = keep.tile([P, S], U8, name="x_bytes")
+        spread = keep.tile([P, H + S], U8, name="spread")
+        planes = keep.tile([P, H + S], U8, name="planes", align_bytes=64)
+        nc.vector.memset(planes[:].bitcast(I32), 0)
+        nc.vector.tensor_copy(d_bytes[:], d_scale_table[:].indirect(kidx_list[:]))
+        nc.vector.tensor_copy(x_bytes[:], x_scale_table[:].indirect(offs_list[:]))
+        nc.vector.tensor_copy(
+            spread[:, :H].rearrange("p (t m) -> p m t", t=PACK), d_bytes[:].rearrange("p (m t) -> p m t", t=PACK)
+        )
+        nc.vector.tensor_copy(spread[:, H:].bitcast(I32), x_bytes[:].bitcast(I32))
+        for j in range(4):
+            nc.scalar.dma_start(planes[j:P:32, :].bitcast(I32), spread[8 * j : P : 32, :].bitcast(I32))
+
+        d_picked = keep.tile([P, H], U32, name="d_picked")
+        d_dealt = keep.tile([P, H], U32, name="d_dealt", align_bytes=64)
+        x_picked = keep.tile([P, S], U32, name="x_picked", align_bytes=64)
+        nc.vector.tensor_copy(d_picked[:], d_word_table[:].bitcast(U32).indirect(kidx_list[:]))
+        dealt_view = d_dealt[:].bitcast(I32).rearrange("p (t m) -> p m t", t=PACK)
+        picked_view = d_picked[:].bitcast(I32).rearrange("p (m t) -> p m t", t=PACK)
+        nc.vector.tensor_copy(dealt_view[:, :, 0:2], picked_view[:, :, 0:2])
+        nc.vector.tensor_copy(x_picked[:], x_word_table[:].bitcast(U32).indirect(offs_list[:]))
+        nc.vector.tensor_copy(dealt_view[:, :, 2:4], picked_view[:, :, 2:4])
+        load_tab(2, "d_word_table")
+        load_tab(3, "x_word_table")
+
+        half_sign = keep.tile([P, PACK], F32, name="half_sign")
+        minus_h32 = keep.tile([P, PACK], F32, name="minus_h32")
+        g_abs = keep.tile([P, PACK], F32, name="g_abs")
+        g_abs16 = keep.tile([P, PACK], F32, name="g_abs16")
+        h_rows = keep.tile([P, PACK, S], F32, name="h_rows")
+        nc.vector.tensor_scalar(half_sign[:], gb_sb[:], 0.0, 0.5, ALU.is_ge, ALU.subtract)
+        nc.vector.scalar_tensor_tensor(minus_h32[:], half_sign[:], -0.0625, ga_sb[:], ALU.mult, ALU.mult)
+        nc.scalar.activation(g_abs[:], gb_sb[:], ACT.Abs)
+        nc.scalar.activation(g_abs16[:], gb_sb[:], ACT.Abs, scale=0.0625)
+        for t in range(PACK):
+            nc.scalar.activation(h_rows[:, t, :], minus_h32[:, t : t + 1].to_broadcast([P, S]), ACT.Copy, scale=-32.0)
+        minus_half = keep.tile([P, W], F32, name="minus_half")
+        nc.gpsimd.memset(minus_half[:], -0.5)
+
+        z_planes = keep.tile([P, PACK, S], BF16, name="z_planes")
+        with_kind = keep.tile([P, PACK, S], F32, name="with_kind")
+        at_place = keep.tile([P, PACK, S], F32, name="at_place")
+        halves = [(slice(c * HALF, (c + 1) * HALF), slice(c * LIST_HALF, (c + 1) * LIST_HALF)) for c in range(2)]
+        acc, rl, gs, kind = {}, {}, {}, {}
+
+        def product(t):
+            acc[t] = psum.tile([P, S], F32, name="s_acc%d" % t)
+            keys = slice(t * P, (t + 1) * P)
+            nc.tensor.matmul_mx(
+                out=acc[t][:],
+                lhsT=d_dealt[:, keys].bitcast(FP8X4),
+                lhsT_scale=planes[:, keys],
+                rhs=x_picked[:].bitcast(FP8X4),
+                rhs_scale=planes[:, H:],
+                start=True,
+                stop=True,
+            )
+
+        def positive_part(t):
+            rl[t] = keep.tile([P, S], F32, name="rl%d" % t)
+            nc.scalar.activation(rl[t][:], acc[t][:], ACT.Relu, scale=0.0625)
+
+        def look_ups(t):
+            gs[t] = keep.tile([P, S], F32, name="gs%d" % t)
+            kind[t] = keep.tile([P, S], F32, name="kind%d" % t)
+            nc.scalar.activation(gs[t][:], acc[t][:], ACT.Copy, scale=g_abs16[:, t : t + 1])
+            for cols, entries in halves:
+                nc.scalar.activation(kind[t][:, cols], tab_sb[t][:].indirect(n2_list[:, entries]), ACT.Copy)
+            for cols, entries in halves:
+                nc.scalar.activation(at_place[:, t, cols], gs[t][:].indirect(n3_list[:, entries]), ACT.Copy)
+
+        def send(t):
+            window = keep.tile([P, 2 * S], F32, name="ds%d" % t)
+            nc.vector.tensor_tensor(window[:].indirect(n1_list[:]), rl[t][:], h_rows[:, t, :], ALU.mult)
+            return window
+
+        def z_rows(t, window):
+            nc.vector.scalar_tensor_tensor(
+                z_planes[:, t, :], acc[t][:], minus_h32[:, t : t + 1], window[:, :S], ALU.mult, ALU.add
+            )
+
+        def add_kind(t):
+            nc.vector.scalar_tensor_tensor(
+                with_kind[:, t, :], kind[t][:], g_abs[:, t : t + 1], gs[t][:], ALU.mult, ALU.add
+            )
+
+        for t in range(PACK):
+            product(t)
+        positive_part(0)
+        ds = {}
+        for t in range(PACK):
+            if t + 1 < PACK:
+                positive_part(t + 1)
+            look_ups(t)
+            ds[t] = send(t)
+            if t > 0:
+                add_kind(t - 1)
+            z_rows(t, ds[t])
+        add_kind(PACK - 1)
+
+        z2_bf = keep.tile([P, S * PACK], BF16, name="z2_bf", align_bytes=64)
+        z2_codes = keep.tile([P, S], U32, name="z2_codes", align_bytes=64)
+        z2_scales = keep.tile([P, S], U8, name="z2_scales", align_bytes=64)
+        z_bf = keep.tile([P, S * PACK], BF16, name="z_bf", align_bytes=64)
+        z_codes = keep.tile([P, S], U32, name="z_codes", align_bytes=64)
+        z_scales = keep.tile([P, S], U8, name="z_scales", align_bytes=64)
+        for c in range(2):
+            nc.scalar.copy(
+                z_bf[:].rearrange("p (u m t) -> p m t u", u=PACK, t=PACK)[:, :, :, 2 * c : 2 * c + 2],
+                z_planes[:].rearrange("p t (m u) -> p m t u", u=PACK)[:, :, :, 2 * c : 2 * c + 2],
+            )
+        nc.vector.tensor_tensor(
+            z2_bf[:].rearrange("p (c i t) -> p c t i", i=4, t=PACK),
+            with_kind[:].rearrange("p t (c i) -> p c t i", i=4),
+            at_place[:].rearrange("p t (c i) -> p c t i", i=4),
+            ALU.max,
+        )
+
+        def quantize_z(c):
+            nc.vector.quantize_mx(
+                out=z_codes[:, c * HALF : (c + 1) * HALF].bitcast(FP8X4),
+                scales=z_scales[:, c * HALF : (c + 1) * HALF],
+                in_=z_bf[:, c * HALF * PACK : (c + 1) * HALF * PACK],
+            )
+
+        quantize_z(0)
+        nc.vector.quantize_mx(out=z2_codes[:].bitcast(FP8X4), scales=z2_scales[:], in_=z2_bf[:])
+        quantize_z(1)
+
+        out_rows = out_0.rearrange("(p u) c -> p u c", u=PACK)
+        pairs = keep.tile([P, 2, S, 2], BF16, name="pairs")
+        out_bf = keep.tile([P, S * PACK], BF16, name="out_bf", align_bytes=64)
+        cm, ra = {}, {}
+        for u in range(PACK):
+            cm_acc = psum.tile([P, S], F32, name="cm_acc%d" % u)
+            rows = slice(u * P, (u + 1) * P)
+            nc.tensor.matmul_mx(
+                out=cm_acc[:],
+                lhsT=z_codes[:, rows].bitcast(FP8X4),
+                lhsT_scale=z_scales[:, rows],
+                rhs=z2_codes[:].bitcast(FP8X4),
+                rhs_scale=z2_scales[:],
+                start=True,
+                stop=True,
+            )
+            cm[u] = keep.tile([P, S], F32, name="cm%d" % u)
+            nc.scalar.activation(cm[u][:], cm_acc[:], ACT.Copy, scale=0.0625)
+
+        def fetch(u):
+            partner = keep.tile([P, W], F32, name="partner%d" % u)
+            ra[u] = keep.tile([P, W], F32, name="ra%d" % u)
+            nc.vector.tensor_tensor(partner[:], cm[u][:].indirect(n5_list[:]), minus_half[:], ALU.mult)
+            nc.vector.tensor_tensor(ra[u][:], cm[u][:].indirect(n4_list[:]), partner[:], ALU.add)
+
+        def put_back(u):
+            if u < PACK - 1:
+                nc.scalar.activation(cm[u][:].indirect(n4_list[:]), ra[u][:], ACT.Copy)
+            else:
+                nc.vector.tensor_copy(cm[u][:].indirect(n4_list[:]), ra[u][:])
+            nc.sync.dma_start(out_rows[:, u, :], cm[u][:])
+
+        def round_rows(u):
+            nc.vector.tensor_copy(pairs[:, u // 2, :, u % 2], cm[u][:])
+
+        for u in range(PACK):
+            fetch(u)
+            if u < PACK - 1:
+                put_back(u)
+        round_rows(0)
+        put_back(PACK - 1)
+        for u in range(1, PACK):
+            round_rows(u)
+        nc.vector.tensor_copy(
+            out_bf[:].bitcast(I32).rearrange("p (c e) -> p c e", e=2),
+            pairs[:].rearrange("p e c i -> p e (c i)").bitcast(I32).rearrange("p e c -> p c e"),
+        )
+
+        out_codes = keep.tile([P, S], U32, name="out_codes", align_bytes=64)
+        out_scales = keep.tile([P, S], U8, name="out_scales", align_bytes=64)
+        nc.vector.quantize_mx(out=out_codes[:].bitcast(FP8X4), scales=out_scales[:], in_=out_bf[:])
+        nc.sync.dma_start(out_1[0].rearrange("p n t -> p (n t)").bitcast(I32), out_codes[:].bitcast(I32))
+        for q in range(4):
+            queue = nc.sync if q % 2 == 0 else nc.scalar
+            queue.dma_start(out_2[0, 4 * q : 4 * q + 4, :].bitcast(I32), out_scales[32 * q : 32 * q + 4, :].bitcast(I32))

@@ -2,7 +2,7 @@ from contextlib import ExitStack
 
 import concourse.mybir as mybir
 
-K, T, S, G, H, J, W = 512, 2048, 512, 2048, 512, 512, 384
+K, S, H, J, W = 512, 512, 512, 512, 384
 FLOPS = 2 * K * H * S + 2 * H * S * S
 
 F32 = mybir.dt.float32
@@ -17,8 +17,12 @@ ACT = mybir.ActivationFunctionType
 
 P = 128
 PACK = 4
-HALF = S // 2
-LIST_HALF = HALF // 16
+QUADRANT = 32
+BLOCK_PARTITIONS = 8
+SIXTEENTH = 0.0625
+WHOLE = slice(0, S)
+HALVES = (slice(0, S // 2), slice(S // 2, S))
+VECTOR_ROUNDS = 384
 
 
 def tile_picked_simksendkindkdif_none_po_kernel(
@@ -37,7 +41,8 @@ def tile_picked_simksendkindkdif_none_po_kernel(
         def load_scale_rows(name, ap):
             tile = keep.tile([P, ap.shape[2]], U8, name=name)
             rows = ap[0].bitcast(I32)
-            nc.sync.dma_start(tile[:].bitcast(I32), rows.unsqueeze(1).to_broadcast([16, 8, rows.shape[1]]))
+            repeated = rows.unsqueeze(1).to_broadcast([rows.shape[0], BLOCK_PARTITIONS, rows.shape[1]])
+            nc.sync.dma_start(tile[:].bitcast(I32), repeated)
             return tile
 
         def load_words(name, ap):
@@ -45,44 +50,63 @@ def tile_picked_simksendkindkdif_none_po_kernel(
             nc.sync.dma_start(tile[:], ap[0].rearrange("p n t -> p (n t)").bitcast(I32))
             return tile
 
+        def load_factor(name, ap):
+            tile = keep.tile([P, PACK], F32, name=name)
+            nc.gpsimd.dma_start(tile[:], ap.rearrange("(p t) o -> p (t o)", t=PACK))
+            return tile
+
+        def product(out, codes, scales, rows, moving_codes, moving_scales):
+            nc.tensor.matmul_mx(
+                out=out,
+                lhsT=codes[:, rows].bitcast(FP8X4),
+                lhsT_scale=scales[:, rows],
+                rhs=moving_codes.bitcast(FP8X4),
+                rhs_scale=moving_scales,
+                start=True,
+                stop=True,
+            )
+
+        def quantize(codes, scales, woven, cols):
+            nc.vector.quantize_mx(
+                out=codes[:, cols].bitcast(FP8X4),
+                scales=scales[:, cols],
+                in_=woven[:, PACK * cols.start : PACK * cols.stop],
+            )
+
+        def scale_rows_on_gpsimd(out, in_, factor):
+            nc.gpsimd.tensor_scalar(out, in_, factor, 0.0, ALU.mult, ALU.add)
+
         kidx_list = load_list("kidx_list", kidx)
         d_scale_table = load_scale_rows("d_scale_table", d_scales)
         offs_list = load_list("offs_list", offs)
         x_scale_table = load_scale_rows("x_scale_table", x_scales)
         d_word_table = load_words("d_word_table", d_words)
-        ga_sb = keep.tile([P, PACK], F32, name="ga_sb")
-        gb_sb = keep.tile([P, PACK], F32, name="gb_sb")
-        nc.sync.dma_start(gb_sb[:], gb.rearrange("(p t) o -> p (t o)", t=PACK))
-        nc.sync.dma_start(ga_sb[:], ga.rearrange("(p t) o -> p (t o)", t=PACK))
+        gb_sb = load_factor("gb_sb", gb)
+        ga_sb = load_factor("ga_sb", ga)
         n1_list = load_list("n1_list", n1)
         n3_list = load_list("n3_list", n3)
-        n2_list = load_list("n2_list", n2)
-        n4_list = load_list("n4_list", n4)
         x_word_table = load_words("x_word_table", x_words)
+        n2_list = load_list("n2_list", n2)
         n5_list = load_list("n5_list", n5)
-        tab_rows = tab.rearrange("(p t) c -> p t c", t=PACK)
-        tab_sb = {}
-
-        def load_tab(t, tag):
-            tab_sb[t] = keep.tile([P, J], F32, name="tab%d" % t, tag=tag)
-            nc.sync.dma_start(tab_sb[t][:], tab_rows[:, t, :])
-
-        load_tab(0, "tab0")
-        load_tab(1, "tab1")
+        n4_list = load_list("n4_list", n4)
 
         d_bytes = keep.tile([P, H], U8, name="d_bytes")
         x_bytes = keep.tile([P, S], U8, name="x_bytes")
-        spread = keep.tile([P, H + S], U8, name="spread")
-        planes = keep.tile([P, H + S], U8, name="planes", align_bytes=64)
-        nc.vector.memset(planes[:].bitcast(I32), 0)
+        both_bytes = keep.tile([P, H + S], U8, name="both_bytes")
+        picked_scales = keep.tile([P, H + S], U8, name="picked_scales", align_bytes=64)
+        nc.vector.memset(picked_scales[:].bitcast(I32), 0)
         nc.vector.tensor_copy(d_bytes[:], d_scale_table[:].indirect(kidx_list[:]))
         nc.vector.tensor_copy(x_bytes[:], x_scale_table[:].indirect(offs_list[:]))
         nc.vector.tensor_copy(
-            spread[:, :H].rearrange("p (t m) -> p m t", t=PACK), d_bytes[:].rearrange("p (m t) -> p m t", t=PACK)
+            both_bytes[:, :H].rearrange("p (t m) -> p m t", t=PACK), d_bytes[:].rearrange("p (m t) -> p m t", t=PACK)
         )
-        nc.vector.tensor_copy(spread[:, H:].bitcast(I32), x_bytes[:].bitcast(I32))
-        for j in range(4):
-            nc.scalar.dma_start(planes[j:P:32, :].bitcast(I32), spread[8 * j : P : 32, :].bitcast(I32))
+        nc.vector.tensor_copy(both_bytes[:, H:].bitcast(I32), x_bytes[:].bitcast(I32))
+        for j in range(QUADRANT // BLOCK_PARTITIONS):
+            nc.scalar.dma_start(
+                picked_scales[j:P:QUADRANT, :].bitcast(I32),
+                both_bytes[BLOCK_PARTITIONS * j : P : QUADRANT, :].bitcast(I32),
+            )
+        x_picked_scales = picked_scales[:, H:]
 
         d_picked = keep.tile([P, H], U32, name="d_picked")
         d_dealt = keep.tile([P, H], U32, name="d_dealt", align_bytes=64)
@@ -91,167 +115,157 @@ def tile_picked_simksendkindkdif_none_po_kernel(
         dealt_view = d_dealt[:].bitcast(I32).rearrange("p (t m) -> p m t", t=PACK)
         picked_view = d_picked[:].bitcast(I32).rearrange("p (m t) -> p m t", t=PACK)
         nc.vector.tensor_copy(dealt_view[:, :, 0:2], picked_view[:, :, 0:2])
-        nc.vector.tensor_copy(x_picked[:], x_word_table[:].bitcast(U32).indirect(offs_list[:]))
+        for cols in HALVES:
+            entries = offs_list[:, cols.start // 16 : cols.stop // 16]
+            nc.vector.tensor_copy(x_picked[:, cols], x_word_table[:].bitcast(U32).indirect(entries))
         nc.vector.tensor_copy(dealt_view[:, :, 2:4], picked_view[:, :, 2:4])
-        load_tab(2, "d_word_table")
-        load_tab(3, "x_word_table")
+
+        tab_rows = tab.rearrange("(p t) c -> p t c", t=PACK)
+        tab_sb = []
+        for t, freed in enumerate(("d_word_table", "both_bytes", "x_word_table", "d_picked")):
+            tab_sb.append(keep.tile([P, 2 * J], F32, name="tab%d" % t, tag=freed))
+            nc.sync.dma_start(tab_sb[t][:, J:], tab_rows[:, t, :])
 
         half_sign = keep.tile([P, PACK], F32, name="half_sign")
+        half_h = keep.tile([P, PACK], F32, name="half_h")
         minus_h32 = keep.tile([P, PACK], F32, name="minus_h32")
+        h16 = keep.tile([P, PACK], F32, name="h16")
         g_abs = keep.tile([P, PACK], F32, name="g_abs")
         g_abs16 = keep.tile([P, PACK], F32, name="g_abs16")
-        h_rows = keep.tile([P, PACK, S], F32, name="h_rows")
-        nc.vector.tensor_scalar(half_sign[:], gb_sb[:], 0.0, 0.5, ALU.is_ge, ALU.subtract)
-        nc.vector.scalar_tensor_tensor(minus_h32[:], half_sign[:], -0.0625, ga_sb[:], ALU.mult, ALU.mult)
+        nc.gpsimd.tensor_scalar(half_sign[:], gb_sb[:], 0.0, 0.5, ALU.is_ge, ALU.subtract)
+        nc.gpsimd.tensor_tensor(half_h[:], half_sign[:], ga_sb[:], ALU.mult)
+        scale_rows_on_gpsimd(minus_h32[:], half_h[:], -SIXTEENTH)
         nc.scalar.activation(g_abs[:], gb_sb[:], ACT.Abs)
-        nc.scalar.activation(g_abs16[:], gb_sb[:], ACT.Abs, scale=0.0625)
-        for t in range(PACK):
-            nc.scalar.activation(h_rows[:, t, :], minus_h32[:, t : t + 1].to_broadcast([P, S]), ACT.Copy, scale=-32.0)
+        nc.scalar.activation(g_abs16[:], gb_sb[:], ACT.Abs, scale=SIXTEENTH)
+        scale_rows_on_gpsimd(h16[:], half_h[:], 2 * SIXTEENTH)
         minus_half = keep.tile([P, W], F32, name="minus_half")
         nc.gpsimd.memset(minus_half[:], -0.5)
 
-        z_planes = keep.tile([P, PACK, S], BF16, name="z_planes")
+        s_acc = [psum.tile([P, S], F32, name="s_acc%d" % t) for t in range(PACK)]
+        for t in range(PACK):
+            for cols in HALVES if t == 0 else (WHOLE,):
+                keys = slice(t * P, (t + 1) * P)
+                product(s_acc[t][:, cols], d_dealt, picked_scales, keys, x_picked[:, cols], x_picked_scales[:, cols])
+
+        gs = [keep.tile([P, 2 * S], F32, name="gs%d" % t) for t in range(PACK)]
+        h_rl = [keep.tile([P, S], F32, name="h_rl%d" % t) for t in range(PACK)]
+        h_ds = [keep.tile([P, 2 * S], F32, name="h_ds%d" % t) for t in range(PACK)]
         with_kind = keep.tile([P, PACK, S], F32, name="with_kind")
         at_place = keep.tile([P, PACK, S], F32, name="at_place")
-        halves = [(slice(c * HALF, (c + 1) * HALF), slice(c * LIST_HALF, (c + 1) * LIST_HALF)) for c in range(2)]
-        acc, rl, gs, kind = {}, {}, {}, {}
+        z_tiles = keep.tile([P, PACK, S], BF16, name="z_tiles")
 
-        def product(t):
-            acc[t] = psum.tile([P, S], F32, name="s_acc%d" % t)
-            keys = slice(t * P, (t + 1) * P)
-            nc.tensor.matmul_mx(
-                out=acc[t][:],
-                lhsT=d_dealt[:, keys].bitcast(FP8X4),
-                lhsT_scale=planes[:, keys],
-                rhs=x_picked[:].bitcast(FP8X4),
-                rhs_scale=planes[:, H:],
-                start=True,
-                stop=True,
-            )
+        nc.vector.tensor_scalar(h_rl[0][:], s_acc[0][:], 0.0, h16[:, 0:1], ALU.max, ALU.mult)
+        for t in range(1, PACK):
+            nc.scalar.activation(gs[t][:, S:], s_acc[t][:], ACT.Relu)
+            scale_rows_on_gpsimd(h_rl[t][:], gs[t][:, S:], h16[:, t : t + 1])
+        for t in range(PACK):
+            scale_rows_on_gpsimd(tab_sb[t][:, :J], tab_sb[t][:, J:], g_abs[:, t : t + 1])
 
-        def positive_part(t):
-            rl[t] = keep.tile([P, S], F32, name="rl%d" % t)
-            nc.scalar.activation(rl[t][:], acc[t][:], ACT.Relu, scale=0.0625)
-
-        def look_ups(t):
-            gs[t] = keep.tile([P, S], F32, name="gs%d" % t)
-            kind[t] = keep.tile([P, S], F32, name="kind%d" % t)
-            nc.scalar.activation(gs[t][:], acc[t][:], ACT.Copy, scale=g_abs16[:, t : t + 1])
-            for cols, entries in halves:
-                nc.scalar.activation(kind[t][:, cols], tab_sb[t][:].indirect(n2_list[:, entries]), ACT.Copy)
-            for cols, entries in halves:
-                nc.scalar.activation(at_place[:, t, cols], gs[t][:].indirect(n3_list[:, entries]), ACT.Copy)
-
-        def send(t):
-            window = keep.tile([P, 2 * S], F32, name="ds%d" % t)
-            nc.vector.tensor_tensor(window[:].indirect(n1_list[:]), rl[t][:], h_rows[:, t, :], ALU.mult)
-            return window
-
-        def z_rows(t, window):
-            nc.vector.scalar_tensor_tensor(
-                z_planes[:, t, :], acc[t][:], minus_h32[:, t : t + 1], window[:, :S], ALU.mult, ALU.add
-            )
-
-        def add_kind(t):
-            nc.vector.scalar_tensor_tensor(
-                with_kind[:, t, :], kind[t][:], g_abs[:, t : t + 1], gs[t][:], ALU.mult, ALU.add
-            )
+        def fetch_places(t):
+            nc.scalar.activation(at_place[:, t, :], gs[t][:].indirect(n3_list[:]), ACT.Copy)
 
         for t in range(PACK):
-            product(t)
-        positive_part(0)
-        ds = {}
-        for t in range(PACK):
-            if t + 1 < PACK:
-                positive_part(t + 1)
-            look_ups(t)
-            ds[t] = send(t)
-            if t > 0:
-                add_kind(t - 1)
-            z_rows(t, ds[t])
-        add_kind(PACK - 1)
+            kind = keep.tile([P, S], F32, name="kind%d" % t)
+            nc.scalar.activation(gs[t][:, :S], s_acc[t][:], ACT.Copy, scale=g_abs16[:, t : t + 1])
+            nc.scalar.activation(kind[:], tab_sb[t][:].indirect(n2_list[:]), ACT.Copy)
+            nc.gpsimd.tensor_tensor(with_kind[:, t, :], kind[:], gs[t][:, :S], ALU.add)
+            nc.vector.tensor_copy(h_ds[t][:].indirect(n1_list[:]), h_rl[t][:])
+            if t == 0:
+                nc.scalar.activation(gs[0][:, S:], s_acc[0][:], ACT.Copy, scale=minus_h32[:, 0:1])
+                nc.gpsimd.tensor_tensor(z_tiles[:, 0, :], h_ds[0][:, :S], gs[0][:, S:], ALU.add)
+            else:
+                fetch_places(t - 1)
+        fetch_places(PACK - 1)
+        for t in range(1, PACK):
+            nc.vector.scalar_tensor_tensor(
+                z_tiles[:, t, :], s_acc[t][:], minus_h32[:, t : t + 1], h_ds[t][:, :S], ALU.mult, ALU.add
+            )
 
-        z2_bf = keep.tile([P, S * PACK], BF16, name="z2_bf", align_bytes=64)
+        z2_woven = keep.tile([P, S * PACK], BF16, name="z2_woven", align_bytes=64)
         z2_codes = keep.tile([P, S], U32, name="z2_codes", align_bytes=64)
         z2_scales = keep.tile([P, S], U8, name="z2_scales", align_bytes=64)
-        z_bf = keep.tile([P, S * PACK], BF16, name="z_bf", align_bytes=64)
+        z_woven = keep.tile([P, S * PACK], BF16, name="z_woven", align_bytes=64)
         z_codes = keep.tile([P, S], U32, name="z_codes", align_bytes=64)
         z_scales = keep.tile([P, S], U8, name="z_scales", align_bytes=64)
-        for c in range(2):
+        for u in (0, 2):
             nc.scalar.copy(
-                z_bf[:].rearrange("p (u m t) -> p m t u", u=PACK, t=PACK)[:, :, :, 2 * c : 2 * c + 2],
-                z_planes[:].rearrange("p t (m u) -> p m t u", u=PACK)[:, :, :, 2 * c : 2 * c + 2],
+                z_woven[:].rearrange("p (u m t) -> p m t u", u=PACK, t=PACK)[:, :, :, u : u + 2],
+                z_tiles[:].rearrange("p t (m u) -> p m t u", u=PACK)[:, :, :, u : u + 2],
             )
         nc.vector.tensor_tensor(
-            z2_bf[:].rearrange("p (c i t) -> p c t i", i=4, t=PACK),
+            z2_woven[:].rearrange("p (c i t) -> p c t i", i=4, t=PACK),
             with_kind[:].rearrange("p t (c i) -> p c t i", i=4),
             at_place[:].rearrange("p t (c i) -> p c t i", i=4),
             ALU.max,
         )
+        quantize(z_codes, z_scales, z_woven, HALVES[0])
+        for cols in HALVES:
+            quantize(z2_codes, z2_scales, z2_woven, cols)
+        quantize(z_codes, z_scales, z_woven, HALVES[1])
 
-        def quantize_z(c):
-            nc.vector.quantize_mx(
-                out=z_codes[:, c * HALF : (c + 1) * HALF].bitcast(FP8X4),
-                scales=z_scales[:, c * HALF : (c + 1) * HALF],
-                in_=z_bf[:, c * HALF * PACK : (c + 1) * HALF * PACK],
-            )
-
-        quantize_z(0)
-        nc.vector.quantize_mx(out=z2_codes[:].bitcast(FP8X4), scales=z2_scales[:], in_=z2_bf[:])
-        quantize_z(1)
+        cm_acc = [psum.tile([P, S], F32, name="cm_acc%d" % u) for u in range(PACK)]
+        for u in range(PACK):
+            for cols in HALVES if u == 0 else (WHOLE,):
+                rows = slice(u * P, (u + 1) * P)
+                product(cm_acc[u][:, cols], z_codes, z_scales, rows, z2_codes[:, cols], z2_scales[:, cols])
 
         out_rows = out_0.rearrange("(p u) c -> p u c", u=PACK)
-        pairs = keep.tile([P, 2, S, 2], BF16, name="pairs")
-        out_bf = keep.tile([P, S * PACK], BF16, name="out_bf", align_bytes=64)
-        cm, ra = {}, {}
-        for u in range(PACK):
-            cm_acc = psum.tile([P, S], F32, name="cm_acc%d" % u)
-            rows = slice(u * P, (u + 1) * P)
-            nc.tensor.matmul_mx(
-                out=cm_acc[:],
-                lhsT=z_codes[:, rows].bitcast(FP8X4),
-                lhsT_scale=z_scales[:, rows],
-                rhs=z2_codes[:].bitcast(FP8X4),
-                rhs_scale=z2_scales[:],
-                start=True,
-                stop=True,
-            )
-            cm[u] = keep.tile([P, S], F32, name="cm%d" % u)
-            nc.scalar.activation(cm[u][:], cm_acc[:], ACT.Copy, scale=0.0625)
+        cm = [keep.tile([P, S], F32, name="cm%d" % u) for u in range(PACK)]
+        partner = [keep.tile([P, W], F32, name="partner%d" % u) for u in range(PACK)]
+        ra = [keep.tile([P, W], F32, name="ra%d" % u) for u in range(PACK)]
 
-        def fetch(u):
-            partner = keep.tile([P, W], F32, name="partner%d" % u)
-            ra[u] = keep.tile([P, W], F32, name="ra%d" % u)
-            nc.vector.tensor_tensor(partner[:], cm[u][:].indirect(n5_list[:]), minus_half[:], ALU.mult)
-            nc.vector.tensor_tensor(ra[u][:], cm[u][:].indirect(n4_list[:]), partner[:], ALU.add)
+        def cm_by_scalar(u):
+            nc.scalar.activation(cm[u][:], cm_acc[u][:], ACT.Copy, scale=SIXTEENTH)
 
-        def put_back(u):
-            if u < PACK - 1:
-                nc.scalar.activation(cm[u][:].indirect(n4_list[:]), ra[u][:], ACT.Copy)
-            else:
-                nc.vector.tensor_copy(cm[u][:].indirect(n4_list[:]), ra[u][:])
+        def partner_by_vector(u):
+            nc.vector.tensor_tensor(partner[u][:], cm[u][:].indirect(n5_list[:]), minus_half[:], ALU.mult)
+
+        def ra_by_vector(u):
+            nc.vector.tensor_tensor(ra[u][:], cm[u][:].indirect(n4_list[:]), partner[u][:], ALU.add)
+
+        def put_back_by_scalar(u):
+            nc.scalar.activation(cm[u][:].indirect(n4_list[:]), ra[u][:], ACT.Copy)
             nc.sync.dma_start(out_rows[:, u, :], cm[u][:])
 
-        def round_rows(u):
-            nc.vector.tensor_copy(pairs[:, u // 2, :, u % 2], cm[u][:])
+        nc.vector.tensor_scalar(cm[0][:], cm_acc[0][:], SIXTEENTH, None, ALU.mult)
+        partner_by_vector(0)
+        cm_by_scalar(1)
+        nc.scalar.activation(partner[1][:], cm[1][:].indirect(n5_list[:]), ACT.Copy, scale=-0.5)
+        ra_by_vector(0)
+        cm_by_scalar(2)
+        cm_by_scalar(3)
+        put_back_by_scalar(0)
+        ra_by_vector(1)
+        put_back_by_scalar(1)
+        partner_by_vector(3)
+        partner_by_vector(2)
+        ra_by_vector(3)
+        ra_by_vector(2)
+        put_back_by_scalar(2)
+        nc.vector.tensor_copy(cm[3][:].indirect(n4_list[:]), ra[3][:])
+        nc.sync.dma_start(out_rows[:, 3, :], cm[3][:])
 
-        for u in range(PACK):
-            fetch(u)
-            if u < PACK - 1:
-                put_back(u)
-        round_rows(0)
-        put_back(PACK - 1)
-        for u in range(1, PACK):
-            round_rows(u)
-        nc.vector.tensor_copy(
-            out_bf[:].bitcast(I32).rearrange("p (c e) -> p c e", e=2),
-            pairs[:].rearrange("p e c i -> p e (c i)").bitcast(I32).rearrange("p e c -> p c e"),
-        )
-
+        pairs = keep.tile([P, 2, S, 2], BF16, name="pairs", tag="partner2")
+        out_woven = keep.tile([P, S * PACK], BF16, name="out_woven", align_bytes=64)
         out_codes = keep.tile([P, S], U32, name="out_codes", align_bytes=64)
         out_scales = keep.tile([P, S], U8, name="out_scales", align_bytes=64)
-        nc.vector.quantize_mx(out=out_codes[:].bitcast(FP8X4), scales=out_scales[:], in_=out_bf[:])
-        nc.sync.dma_start(out_1[0].rearrange("p n t -> p (n t)").bitcast(I32), out_codes[:].bitcast(I32))
-        for q in range(4):
-            queue = nc.sync if q % 2 == 0 else nc.scalar
-            queue.dma_start(out_2[0, 4 * q : 4 * q + 4, :].bitcast(I32), out_scales[32 * q : 32 * q + 4, :].bitcast(I32))
+        for u in (0, 1):
+            scale_rows_on_gpsimd(pairs[:, 0, :, u], cm[u][:], 1.0)
+        for copy, cols in ((nc.vector.tensor_copy, slice(0, VECTOR_ROUNDS)), (nc.scalar.copy, slice(VECTOR_ROUNDS, S))):
+            for u in (3, 2):
+                copy(pairs[:, 1, cols, u - 2], cm[u][:, cols])
+        for copy, word, cols in ((nc.vector.tensor_copy, I32, HALVES[0]), (nc.scalar.copy, U32, HALVES[1])):
+            copy(
+                out_woven[:].bitcast(word).rearrange("p (c e) -> p c e", e=2)[:, cols, :],
+                pairs[:].rearrange("p e c i -> p e (c i)").bitcast(word).rearrange("p e c -> p c e")[:, cols, :],
+            )
+        out_words = out_1[0].rearrange("p n t -> p (n t)").bitcast(I32)
+        for cols in HALVES:
+            quantize(out_codes, out_scales, out_woven, cols)
+            nc.sync.dma_start(out_words[:, cols], out_codes[:, cols].bitcast(I32))
+        for q in range(P // QUADRANT):
+            queue = nc.sync if q == 3 else nc.scalar
+            queue.dma_start(
+                out_2[0, 4 * q : 4 * q + 4, :].bitcast(I32),
+                out_scales[QUADRANT * q : QUADRANT * q + 4, :].bitcast(I32),
+            )

from contextlib import ExitStack

import concourse.mybir as mybir

K, S, H, J, W = 512, 512, 512, 512, 384
FLOPS = 2 * K * H * S + 2 * H * S * S

F32 = mybir.dt.float32
BF16 = mybir.dt.bfloat16
I32 = mybir.dt.int32
U32 = mybir.dt.uint32
U16 = mybir.dt.uint16
U8 = mybir.dt.uint8
FP8X4 = mybir.dt.float8_e4m3fn_x4
ALU = mybir.AluOpType
ACT = mybir.ActivationFunctionType

P = 128
PACK = 4
QUADRANT = 32
BLOCK_PARTITIONS = 8
SIXTEENTH = 0.0625
WHOLE = slice(0, S)
HALVES = (slice(0, S // 2), slice(S // 2, S))
VECTOR_ROUNDS = 384


def tile_picked_simksendkindkdif_none_po_kernel(
    tc, x_words, x_scales, d_words, d_scales, tab, ga, gb, offs, kidx, n1, n2, n3, n4, n5, out_0, out_1, out_2
):
    nc = tc.nc
    with ExitStack() as ctx:
        keep = ctx.enter_context(tc.tile_pool(name="keep", bufs=1))
        psum = ctx.enter_context(tc.psum_pool(name="psum", bufs=1))

        def load_list(name, ap):
            tile = keep.tile(list(ap.shape), U16, name=name)
            nc.sync.dma_start(tile[:], ap)
            return tile

        def load_scale_rows(name, ap):
            tile = keep.tile([P, ap.shape[2]], U8, name=name)
            rows = ap[0].bitcast(I32)
            repeated = rows.unsqueeze(1).to_broadcast([rows.shape[0], BLOCK_PARTITIONS, rows.shape[1]])
            nc.sync.dma_start(tile[:].bitcast(I32), repeated)
            return tile

        def load_words(name, ap):
            tile = keep.tile([P, ap.shape[2]], I32, name=name)
            nc.sync.dma_start(tile[:], ap[0].rearrange("p n t -> p (n t)").bitcast(I32))
            return tile

        def load_factor(name, ap):
            tile = keep.tile([P, PACK], F32, name=name)
            nc.gpsimd.dma_start(tile[:], ap.rearrange("(p t) o -> p (t o)", t=PACK))
            return tile

        def product(out, codes, scales, rows, moving_codes, moving_scales):
            nc.tensor.matmul_mx(
                out=out,
                lhsT=codes[:, rows].bitcast(FP8X4),
                lhsT_scale=scales[:, rows],
                rhs=moving_codes.bitcast(FP8X4),
                rhs_scale=moving_scales,
                start=True,
                stop=True,
            )

        def quantize(codes, scales, woven, cols):
            nc.vector.quantize_mx(
                out=codes[:, cols].bitcast(FP8X4),
                scales=scales[:, cols],
                in_=woven[:, PACK * cols.start : PACK * cols.stop],
            )

        def scale_rows_on_gpsimd(out, in_, factor):
            nc.gpsimd.tensor_scalar(out, in_, factor, 0.0, ALU.mult, ALU.add)

        kidx_list = load_list("kidx_list", kidx)
        d_scale_table = load_scale_rows("d_scale_table", d_scales)
        offs_list = load_list("offs_list", offs)
        x_scale_table = load_scale_rows("x_scale_table", x_scales)
        d_word_table = load_words("d_word_table", d_words)
        gb_sb = load_factor("gb_sb", gb)
        ga_sb = load_factor("ga_sb", ga)
        n1_list = load_list("n1_list", n1)
        n3_list = load_list("n3_list", n3)
        x_word_table = load_words("x_word_table", x_words)
        n2_list = load_list("n2_list", n2)
        n5_list = load_list("n5_list", n5)
        n4_list = load_list("n4_list", n4)

        d_bytes = keep.tile([P, H], U8, name="d_bytes")
        x_bytes = keep.tile([P, S], U8, name="x_bytes")
        both_bytes = keep.tile([P, H + S], U8, name="both_bytes")
        picked_scales = keep.tile([P, H + S], U8, name="picked_scales", align_bytes=64)
        nc.vector.memset(picked_scales[:].bitcast(I32), 0)
        nc.vector.tensor_copy(d_bytes[:], d_scale_table[:].indirect(kidx_list[:]))
        nc.vector.tensor_copy(x_bytes[:], x_scale_table[:].indirect(offs_list[:]))
        nc.vector.tensor_copy(
            both_bytes[:, :H].rearrange("p (t m) -> p m t", t=PACK), d_bytes[:].rearrange("p (m t) -> p m t", t=PACK)
        )
        nc.vector.tensor_copy(both_bytes[:, H:].bitcast(I32), x_bytes[:].bitcast(I32))
        for j in range(QUADRANT // BLOCK_PARTITIONS):
            nc.scalar.dma_start(
                picked_scales[j:P:QUADRANT, :].bitcast(I32),
                both_bytes[BLOCK_PARTITIONS * j : P : QUADRANT, :].bitcast(I32),
            )
        x_picked_scales = picked_scales[:, H:]

        d_picked = keep.tile([P, H], U32, name="d_picked")
        d_dealt = keep.tile([P, H], U32, name="d_dealt", align_bytes=64)
        x_picked = keep.tile([P, S], U32, name="x_picked", align_bytes=64)
        nc.vector.tensor_copy(d_picked[:], d_word_table[:].bitcast(U32).indirect(kidx_list[:]))
        dealt_view = d_dealt[:].bitcast(I32).rearrange("p (t m) -> p m t", t=PACK)
        picked_view = d_picked[:].bitcast(I32).rearrange("p (m t) -> p m t", t=PACK)
        nc.vector.tensor_copy(dealt_view[:, :, 0:2], picked_view[:, :, 0:2])
        for cols in HALVES:
            entries = offs_list[:, cols.start // 16 : cols.stop // 16]
            nc.vector.tensor_copy(x_picked[:, cols], x_word_table[:].bitcast(U32).indirect(entries))
        nc.vector.tensor_copy(dealt_view[:, :, 2:4], picked_view[:, :, 2:4])

        tab_rows = tab.rearrange("(p t) c -> p t c", t=PACK)
        tab_sb = []
        for t, freed in enumerate(("d_word_table", "both_bytes", "x_word_table", "d_picked")):
            tab_sb.append(keep.tile([P, 2 * J], F32, name="tab%d" % t, tag=freed))
            nc.sync.dma_start(tab_sb[t][:, J:], tab_rows[:, t, :])

        half_sign = keep.tile([P, PACK], F32, name="half_sign")
        half_h = keep.tile([P, PACK], F32, name="half_h")
        minus_h32 = keep.tile([P, PACK], F32, name="minus_h32")
        h16 = keep.tile([P, PACK], F32, name="h16")
        g_abs = keep.tile([P, PACK], F32, name="g_abs")
        g_abs16 = keep.tile([P, PACK], F32, name="g_abs16")
        nc.gpsimd.tensor_scalar(half_sign[:], gb_sb[:], 0.0, 0.5, ALU.is_ge, ALU.subtract)
        nc.gpsimd.tensor_tensor(half_h[:], half_sign[:], ga_sb[:], ALU.mult)
        scale_rows_on_gpsimd(minus_h32[:], half_h[:], -SIXTEENTH)
        nc.scalar.activation(g_abs[:], gb_sb[:], ACT.Abs)
        nc.scalar.activation(g_abs16[:], gb_sb[:], ACT.Abs, scale=SIXTEENTH)
        scale_rows_on_gpsimd(h16[:], half_h[:], 2 * SIXTEENTH)
        minus_half = keep.tile([P, W], F32, name="minus_half")
        nc.gpsimd.memset(minus_half[:], -0.5)

        s_acc = [psum.tile([P, S], F32, name="s_acc%d" % t) for t in range(PACK)]
        for t in range(PACK):
            for cols in HALVES if t == 0 else (WHOLE,):
                keys = slice(t * P, (t + 1) * P)
                product(s_acc[t][:, cols], d_dealt, picked_scales, keys, x_picked[:, cols], x_picked_scales[:, cols])

        gs = [keep.tile([P, 2 * S], F32, name="gs%d" % t) for t in range(PACK)]
        h_rl = [keep.tile([P, S], F32, name="h_rl%d" % t) for t in range(PACK)]
        h_ds = [keep.tile([P, 2 * S], F32, name="h_ds%d" % t) for t in range(PACK)]
        with_kind = keep.tile([P, PACK, S], F32, name="with_kind")
        at_place = keep.tile([P, PACK, S], F32, name="at_place")
        z_tiles = keep.tile([P, PACK, S], BF16, name="z_tiles")

        nc.vector.tensor_scalar(h_rl[0][:], s_acc[0][:], 0.0, h16[:, 0:1], ALU.max, ALU.mult)
        for t in range(1, PACK):
            nc.scalar.activation(gs[t][:, S:], s_acc[t][:], ACT.Relu)
            scale_rows_on_gpsimd(h_rl[t][:], gs[t][:, S:], h16[:, t : t + 1])
        for t in range(PACK):
            scale_rows_on_gpsimd(tab_sb[t][:, :J], tab_sb[t][:, J:], g_abs[:, t : t + 1])

        def fetch_places(t):
            nc.scalar.activation(at_place[:, t, :], gs[t][:].indirect(n3_list[:]), ACT.Copy)

        for t in range(PACK):
            kind = keep.tile([P, S], F32, name="kind%d" % t)
            nc.scalar.activation(gs[t][:, :S], s_acc[t][:], ACT.Copy, scale=g_abs16[:, t : t + 1])
            nc.scalar.activation(kind[:], tab_sb[t][:].indirect(n2_list[:]), ACT.Copy)
            nc.gpsimd.tensor_tensor(with_kind[:, t, :], kind[:], gs[t][:, :S], ALU.add)
            nc.vector.tensor_copy(h_ds[t][:].indirect(n1_list[:]), h_rl[t][:])
            if t == 0:
                nc.scalar.activation(gs[0][:, S:], s_acc[0][:], ACT.Copy, scale=minus_h32[:, 0:1])
                nc.gpsimd.tensor_tensor(z_tiles[:, 0, :], h_ds[0][:, :S], gs[0][:, S:], ALU.add)
            else:
                fetch_places(t - 1)
        fetch_places(PACK - 1)
        for t in range(1, PACK):
            nc.vector.scalar_tensor_tensor(
                z_tiles[:, t, :], s_acc[t][:], minus_h32[:, t : t + 1], h_ds[t][:, :S], ALU.mult, ALU.add
            )

        z2_woven = keep.tile([P, S * PACK], BF16, name="z2_woven", align_bytes=64)
        z2_codes = keep.tile([P, S], U32, name="z2_codes", align_bytes=64)
        z2_scales = keep.tile([P, S], U8, name="z2_scales", align_bytes=64)
        z_woven = keep.tile([P, S * PACK], BF16, name="z_woven", align_bytes=64)
        z_codes = keep.tile([P, S], U32, name="z_codes", align_bytes=64)
        z_scales = keep.tile([P, S], U8, name="z_scales", align_bytes=64)
        for u in (0, 2):
            nc.scalar.copy(
                z_woven[:].rearrange("p (u m t) -> p m t u", u=PACK, t=PACK)[:, :, :, u : u + 2],
                z_tiles[:].rearrange("p t (m u) -> p m t u", u=PACK)[:, :, :, u : u + 2],
            )
        nc.vector.tensor_tensor(
            z2_woven[:].rearrange("p (c i t) -> p c t i", i=4, t=PACK),
            with_kind[:].rearrange("p t (c i) -> p c t i", i=4),
            at_place[:].rearrange("p t (c i) -> p c t i", i=4),
            ALU.max,
        )
        quantize(z_codes, z_scales, z_woven, HALVES[0])
        for cols in HALVES:
            quantize(z2_codes, z2_scales, z2_woven, cols)
        quantize(z_codes, z_scales, z_woven, HALVES[1])

        cm_acc = [psum.tile([P, S], F32, name="cm_acc%d" % u) for u in range(PACK)]
        for u in range(PACK):
            for cols in HALVES if u == 0 else (WHOLE,):
                rows = slice(u * P, (u + 1) * P)
                product(cm_acc[u][:, cols], z_codes, z_scales, rows, z2_codes[:, cols], z2_scales[:, cols])

        out_rows = out_0.rearrange("(p u) c -> p u c", u=PACK)
        cm = [keep.tile([P, S], F32, name="cm%d" % u) for u in range(PACK)]
        partner = [keep.tile([P, W], F32, name="partner%d" % u) for u in range(PACK)]
        ra = [keep.tile([P, W], F32, name="ra%d" % u) for u in range(PACK)]

        def cm_by_scalar(u):
            nc.scalar.activation(cm[u][:], cm_acc[u][:], ACT.Copy, scale=SIXTEENTH)

        def partner_by_vector(u):
            nc.vector.tensor_tensor(partner[u][:], cm[u][:].indirect(n5_list[:]), minus_half[:], ALU.mult)

        def ra_by_vector(u):
            nc.vector.tensor_tensor(ra[u][:], cm[u][:].indirect(n4_list[:]), partner[u][:], ALU.add)

        def put_back_by_scalar(u):
            nc.scalar.activation(cm[u][:].indirect(n4_list[:]), ra[u][:], ACT.Copy)
            nc.sync.dma_start(out_rows[:, u, :], cm[u][:])

        nc.vector.tensor_scalar(cm[0][:], cm_acc[0][:], SIXTEENTH, None, ALU.mult)
        partner_by_vector(0)
        cm_by_scalar(1)
        nc.scalar.activation(partner[1][:], cm[1][:].indirect(n5_list[:]), ACT.Copy, scale=-0.5)
        ra_by_vector(0)
        cm_by_scalar(2)
        cm_by_scalar(3)
        put_back_by_scalar(0)
        ra_by_vector(1)
        put_back_by_scalar(1)
        partner_by_vector(3)
        partner_by_vector(2)
        ra_by_vector(3)
        ra_by_vector(2)
        put_back_by_scalar(2)
        nc.vector.tensor_copy(cm[3][:].indirect(n4_list[:]), ra[3][:])
        nc.sync.dma_start(out_rows[:, 3, :], cm[3][:])

        pairs = keep.tile([P, 2, S, 2], BF16, name="pairs", tag="partner2")
        out_woven = keep.tile([P, S * PACK], BF16, name="out_woven", align_bytes=64)
        out_codes = keep.tile([P, S], U32, name="out_codes", align_bytes=64)
        out_scales = keep.tile([P, S], U8, name="out_scales", align_bytes=64)
        for u in (0, 1):
            scale_rows_on_gpsimd(pairs[:, 0, :, u], cm[u][:], 1.0)
        for copy, cols in ((nc.vector.tensor_copy, slice(0, VECTOR_ROUNDS)), (nc.scalar.copy, slice(VECTOR_ROUNDS, S))):
            for u in (3, 2):
                copy(pairs[:, 1, cols, u - 2], cm[u][:, cols])
        for copy, word, cols in ((nc.vector.tensor_copy, I32, HALVES[0]), (nc.scalar.copy, U32, HALVES[1])):
            copy(
                out_woven[:].bitcast(word).rearrange("p (c e) -> p c e", e=2)[:, cols, :],
                pairs[:].rearrange("p e c i -> p e (c i)").bitcast(word).rearrange("p e c -> p c e")[:, cols, :],
            )
        out_words = out_1[0].rearrange("p n t -> p (n t)").bitcast(I32)
        for cols in HALVES:
            quantize(out_codes, out_scales, out_woven, cols)
            nc.sync.dma_start(out_words[:, cols], out_codes[:, cols].bitcast(I32))
        for q in range(P // QUADRANT):
            queue = nc.sync if q == 3 else nc.scalar
            queue.dma_start(
                out_2[0, 4 * q : 4 * q + 4, :].bitcast(I32),
                out_scales[QUADRANT * q : QUADRANT * q + 4, :].bitcast(I32),
            )
